import numpy as np
import ml_dtypes


def mxq(x, axis, fmt="e4m3"):
    dtype, down = {"e4m3": (ml_dtypes.float8_e4m3fn, 7), "e5m2": (ml_dtypes.float8_e5m2, 14)}[fmt]
    v = np.moveaxis(np.asarray(x, np.float32).astype(ml_dtypes.bfloat16).astype(np.float64), axis, -1)
    blocks = v.reshape(v.shape[:-1] + (-1, 32))
    amax = np.abs(blocks).max(-1, keepdims=True)
    byte = np.maximum(np.where(amax > 0, np.frexp(amax)[1] - 1 + 127, 0) - down, 1)
    scale = np.exp2(byte - 127.0)
    codes = (blocks / scale).astype(np.float32).astype(dtype).astype(np.float64)
    return np.moveaxis((codes * scale).reshape(v.shape), -1, axis)


WIDE = False


def mx_kscale(k):
    if not WIDE:
        return np.ones(k)
    levels = np.array([10, -10, 5, -5, 0])
    if k % 512:
        return np.exp2(np.random.permutation(np.resize(levels, k // 32))).repeat(32)
    a = np.empty((k // 512, 16))
    for p in range(k // 512):
        a[p, :8] = np.random.permutation(np.resize(levels, 8))
        for g in range(8):
            far = levels[np.abs(levels - a[p, g]) >= 10]
            a[p, g + 8] = far[np.random.randint(len(far))]
    return np.exp2(a.ravel()).repeat(32)


def f64(x):
    return np.asarray(x).astype(np.float64)


def striped(idx):
    return np.tile(idx.reshape(-1, 16).T, (8, 1)).astype(np.uint16)


def unstriped(offs):
    return offs[:16].T.reshape(-1).astype(np.int64)


def pack_weight(w):
    k, n = w.shape
    w = f64(np.asarray(w, np.float32).astype(ml_dtypes.bfloat16)).reshape(k // 32, 32, n)
    amax = np.abs(w).max(1)
    byte = np.clip(np.where(amax > 0, np.frexp(amax)[1] - 1 + 127 - 7, 1), 1, 254)
    scaled = (w * np.exp2(127.0 - byte)[:, None, :]).reshape(k, n).astype(np.float32)
    words = np.ascontiguousarray(scaled.reshape(k // 512, 128, 4, n).transpose(0, 1, 3, 2)).astype(ml_dtypes.float8_e4m3fn).view(np.uint8)
    return words, np.ascontiguousarray(byte.astype(np.uint8).reshape(k // 512, 16, n))


def unpack_weight(words, scales):
    g, p, n, _ = words.shape
    vals = np.ascontiguousarray(words).view(ml_dtypes.float8_e4m3fn).astype(np.float64) * np.repeat(np.exp2(scales.astype(np.float64) - 127.0), 8, axis=1)[..., None]
    return vals.transpose(0, 1, 3, 2).reshape(g * 512, n)


K, T, S, H, V, W = 1024, 2048, 512, 512, 512, 2048
P = 2 ** 7


def setup_inputs():
    n = np.random.standard_normal
    s = mx_kscale(K)[:, None]
    u = mx_kscale(H)
    packed_xT = pack_weight(n((K, T)) * s)
    packed_eT = pack_weight(n((H, W)) / np.sqrt(H) / u[:, None])
    return {
        "x_words": packed_xT[0],
        "x_scales": packed_xT[1],
        "w1": (n((K, H)) / np.sqrt(K) / s * u).astype(np.float32),
        "e_words": packed_eT[0],
        "e_scales": packed_eT[1],
        "nn": (np.tile(np.random.uniform(1.5, 3.0, W), (P, 1))).astype(np.float32),
        "own": (np.random.uniform(1.5, 3.0, (S, 1))).astype(np.float32),
        "one": (np.tile(np.random.uniform(0.8, 1.2, V), (P, 1))).astype(np.float32),
        "pij": (np.random.uniform(0.0, 1.0, (S, V)) ** 2 * 3).astype(np.float32),
        "offs": striped(np.random.permutation(T)[:S]),
        "lmk": striped(np.random.permutation(W)[:V]),
    }


def reference(x_words, x_scales, w1, e_words, e_scales, nn, own, one, pij, offs, lmk):
    xq = unpack_weight(x_words, x_scales)[:, unstriped(offs)]
    h = mxq(f64(w1), 0, "e4m3").T @ xq
    e_lmk = unpack_weight(e_words, e_scales)[:, unstriped(lmk)]
    y = mxq(h, 0, "e4m3").T @ e_lmk
    dsq = f64(nn)[:1][:, unstriped(lmk)] - (0.6 * y) + f64(own)
    qn = f64(one)[:1] / (dsq + 1.0)
    qm = qn.mean(axis=1, keepdims=True)
    qr = qn / qm
    return (f64(pij) - qr) * qn

@@ -1,0 +1,195 @@
+from contextlib import ExitStack
+
+import concourse.mybir as mybir
+from concourse.masks import make_identity
+
+K, T, S, H, V, W = 1024, 2048, 512, 512, 512, 2048
+FLOPS = 2 * K * H * S + 2 * H * S * V
+
+F32 = mybir.dt.float32
+BF16 = mybir.dt.bfloat16
+I32 = mybir.dt.int32
+U32 = mybir.dt.uint32
+U16 = mybir.dt.uint16
+U8 = mybir.dt.uint8
+FP8X4 = mybir.dt.float8_e4m3fn_x4
+ALU = mybir.AluOpType
+ACT = mybir.ActivationFunctionType
+
+P = 128
+PACK = 4
+PASSES = K // (P * PACK)
+BLOCKS = S // P
+HALF = S // 2
+LIST_ROWS = 16
+INV = 1.0 / 0.6
+
+
+def tile_picked_ytsneg_grad_p_kernel(
+    tc, x_words, x_scales, w1, e_words, e_scales, nn, own, one, pij, offs, lmk, out
+):
+    nc = tc.nc
+    with ExitStack() as ctx:
+        keep = ctx.enter_context(tc.tile_pool(name="keep", bufs=1))
+        work = ctx.enter_context(tc.tile_pool(name="work", bufs=4))
+        psum_h = ctx.enter_context(tc.psum_pool(name="psum_h", bufs=3))
+        psum_y = ctx.enter_context(tc.psum_pool(name="psum_y", bufs=3))
+        psum_n = ctx.enter_context(tc.psum_pool(name="psum_n", bufs=1))
+
+        offs_sb = keep.tile([P, S // LIST_ROWS], U16, name="offs_sb")
+        lmk_sb = keep.tile([P, V // LIST_ROWS], U16, name="lmk_sb")
+        x_scale_table = keep.tile([P, T], U8, name="x_scale_table")
+        e_scale_table = keep.tile([P, W], U8, name="e_scale_table")
+        nn_table = keep.tile([P, W], F32, name="nn_table")
+        nc.vector.memset(x_scale_table[:].bitcast(I32), 0)
+        nc.vector.memset(e_scale_table[:].bitcast(I32), 0)
+        nc.vector.memset(nn_table[:], 0.0)
+        own_rows = keep.tile([P, P], F32, name="own_rows")
+        nc.vector.memset(own_rows[:], 0.0)
+
+        warm = keep.tile([P, 8], F32, name="warm")
+        nc.vector.memset(warm[:], 1.0)
+        nc.scalar.activation(warm[:, 1:2], warm[:, 0:1], ACT.Abs_reciprocal_sqrt)
+
+        w_raw = [keep.tile([P, PACK, H], F32, name="w_raw%d" % g) for g in range(PASSES)]
+        x_table = [keep.tile([P, T], I32, name="x_table%d" % g) for g in range(PASSES)]
+        e_table = keep.tile([P, W], I32, name="e_table")
+        one_sb = keep.tile([P, V], F32, name="one_sb")
+        pij_sb = [keep.tile([P, V], F32, name="pij_sb%d" % b) for b in range(BLOCKS)]
+
+        def load_w(g):
+            rows = w1[g * P * PACK : (g + 1) * P * PACK, :]
+            nc.sync.dma_start(out=w_raw[g][:], in_=rows.rearrange("(p j) c -> p j c", j=PACK))
+
+        load_w(0)
+        for q in range(4):
+            nc.sync.dma_start(
+                out=x_scale_table[32 * q : 32 * q + 4 * PASSES, :].bitcast(I32),
+                in_=x_scales[:, 4 * q : 4 * q + 4, :].bitcast(I32),
+            )
+        nc.sync.dma_start(offs_sb[:], offs)
+        nc.sync.dma_start(lmk_sb[:], lmk)
+        load_w(1)
+        for g in range(PASSES):
+            nc.sync.dma_start(out=x_table[g][:], in_=x_words[g].rearrange("p n t -> p (n t)").bitcast(I32))
+        nc.sync.dma_start(out=e_table[:], in_=e_words[0].rearrange("p n t -> p (n t)").bitcast(I32))
+        nc.sync.dma_start(out=one_sb[:], in_=one)
+        for b in range(BLOCKS):
+            nc.sync.dma_start(out=pij_sb[b][:], in_=pij[b * P : (b + 1) * P, :])
+        nc.gpsimd.dma_start(out=nn_table[0:1, :], in_=nn[0:1, :])
+        nc.gpsimd.dma_start(out=own_rows[0:BLOCKS, :], in_=own.rearrange("(b p) o -> b (p o)", p=P))
+        for q in range(4):
+            nc.gpsimd.dma_start(
+                out=e_scale_table[32 * q : 32 * q + 4, :].bitcast(I32),
+                in_=e_scales[0, 4 * q : 4 * q + 4, :].bitcast(I32),
+            )
+
+        ident = keep.tile([P, P], F32, name="ident")
+        make_identity(nc, ident[:])
+
+        w_codes, w_scales = [], []
+        for g in range(PASSES):
+            grouped = keep.tile([P, PACK * H], BF16, name="w_grouped%d" % g, align_bytes=64)
+            nc.scalar.copy(
+                out=grouped[:].rearrange("p (t m j) -> p m j t", t=PACK, j=PACK),
+                in_=w_raw[g][:].rearrange("p j (m t) -> p m j t", t=PACK),
+            )
+            codes = keep.tile([P, H], U32, name="w_codes%d" % g, align_bytes=64)
+            scales = keep.tile([P, H], U8, name="w_scales%d" % g, align_bytes=64)
+            nc.vector.quantize_mx(out=codes[:].bitcast(FP8X4), scales=scales[:], in_=grouped[:])
+            w_codes.append(codes)
+            w_scales.append(scales)
+
+        x_scale_picked = keep.tile([P, S], U8, name="x_scale_picked", align_bytes=64)
+        nc.vector.tensor_copy(x_scale_picked[:], x_scale_table[:].indirect(offs_sb[:]))
+        e_scale_picked = keep.tile([P, V], U8, name="e_scale_picked", align_bytes=64)
+        nc.vector.tensor_copy(e_scale_picked[:], e_scale_table[:].indirect(lmk_sb[:]))
+
+        nn_row = keep.tile([P, V], F32, name="nn_row")
+        nc.vector.tensor_copy(nn_row[:], nn_table[:].indirect(lmk_sb[:]))
+        nn_turned = psum_n.tile([P, V // P, P], F32, name="nn_turned")
+        for j in range(V // P):
+            nc.tensor.transpose(nn_turned[:, j, :], nn_row[:, j * P : (j + 1) * P], ident[:])
+        nn_col = keep.tile([P, V // P], F32, name="nn_col")
+        nc.vector.tensor_scalar(nn_col[:], nn_turned[:, :, 0], -INV, -INV, ALU.mult, ALU.add)
+        nn_spread = psum_n.tile([P, V], F32, name="nn_spread")
+        for j in range(V // P):
+            nc.tensor.transpose(
+                nn_spread[:, j * P : (j + 1) * P], nn_col[:, j : j + 1].to_broadcast([P, P]), ident[:]
+            )
+        nn_term = keep.tile([P, V], F32, name="nn_term")
+        nc.scalar.copy(out=nn_term[:], in_=nn_spread[:])
+        own_term = keep.tile([P, BLOCKS], F32, name="own_term")
+        own_turned = psum_h.tile([P, PACK, P], F32, name="h_acc")
+        nc.tensor.transpose(own_turned[:, 0, :], own_rows[:], ident[:])
+        nc.vector.tensor_scalar(own_term[:], own_turned[:, 0, 0:BLOCKS], -INV, None, ALU.mult)
+
+        x_picked = {}
+        for g in range(PASSES):
+            for half in range(2):
+                picked = keep.tile([P, HALF], U32, name="x_picked%d%d" % (g, half), align_bytes=64)
+                cols = slice(half * HALF // LIST_ROWS, (half + 1) * HALF // LIST_ROWS)
+                nc.vector.tensor_copy(picked[:], x_table[g][:].bitcast(U32).indirect(offs_sb[:, cols]))
+                x_picked[g, half] = picked
+
+        h_codes, h_scales = [], []
+        for b in range(BLOCKS):
+            half, first = divmod(b * P, HALF)
+            h_acc = psum_h.tile([P, PACK, P], F32, name="h_acc")
+            for t in range(PACK):
+                for g in range(PASSES):
+                    nc.tensor.matmul_mx(
+                        out=h_acc[:, t, :],
+                        lhsT=w_codes[g][:, t * P : (t + 1) * P].bitcast(FP8X4),
+                        lhsT_scale=w_scales[g][:, t * P : (t + 1) * P],
+                        rhs=x_picked[g, half][:, first : first + P].bitcast(FP8X4),
+                        rhs_scale=x_scale_picked[4 * g : P, b * P : (b + 1) * P],
+                        start=(g == 0),
+                        stop=(g == PASSES - 1),
+                    )
+            h_grouped = work.tile([P, P * PACK], BF16, name="h_grouped", align_bytes=64)
+            nc.scalar.copy(
+                out=h_grouped[:].rearrange("p (n t) -> p n t", t=PACK), in_=h_acc[:].rearrange("p t n -> p n t")
+            )
+            codes = work.tile([P, P], U32, name="h_codes", align_bytes=64)
+            scales = work.tile([P, P], U8, name="h_scales", align_bytes=64)
+            nc.vector.quantize_mx(out=codes[:].bitcast(FP8X4), scales=scales[:], in_=h_grouped[:])
+            h_codes.append(codes)
+            h_scales.append(scales)
+
+        e_picked = keep.tile([P, V], U32, name="e_picked", align_bytes=64)
+        nc.vector.tensor_copy(e_picked[:], e_table[:].bitcast(U32).indirect(lmk_sb[:]))
+
+        for b in range(BLOCKS):
+            y_acc = psum_y.tile([P, V], F32, name="y_acc")
+            nc.tensor.matmul_mx(
+                out=y_acc[:],
+                lhsT=h_codes[b][:].bitcast(FP8X4),
+                lhsT_scale=h_scales[b][:],
+                rhs=e_picked[:].bitcast(FP8X4),
+                rhs_scale=e_scale_picked[:],
+                start=True,
+                stop=True,
+            )
+            den = work.tile([P, V], F32, name="den")
+            nc.vector.scalar_tensor_tensor(den[:], y_acc[:], own_term[:, b : b + 1], nn_term[:], ALU.add, ALU.add)
+            sign = work.tile([P, V], F32, name="sign")
+            nc.scalar.activation(sign[:], den[:], ACT.Sign, scale=-1.0)
+            root = work.tile([P, V], F32, name="root")
+            nc.scalar.activation(root[:], den[:], ACT.Abs_reciprocal_sqrt, scale=0.6)
+            inv_abs = work.tile([P, V], F32, name="inv_abs")
+            nc.scalar.activation(inv_abs[:], root[:], ACT.Square)
+            signed_one = work.tile([P, V], F32, name="signed_one")
+            nc.vector.tensor_tensor(signed_one[:], sign[:], one_sb[:], ALU.mult)
+            qn = work.tile([P, V], F32, name="qn")
+            stats = work.tile([P, 8], F32, name="stats")
+            nc.vector.scalar_tensor_tensor(
+                qn[:], signed_one[:], 1.0, inv_abs[:], ALU.mult, ALU.mult, accum_out=stats[:, 0:1]
+            )
+            nc.vector.tensor_scalar(stats[:, 1:2], stats[:, 0:1], -1.0 / V, None, ALU.mult)
+            nc.vector.reciprocal(stats[:, 2:3], stats[:, 1:2])
+            diff = work.tile([P, V], F32, name="diff")
+            nc.vector.scalar_tensor_tensor(diff[:], qn[:], stats[:, 2:3], pij_sb[b][:], ALU.mult, ALU.add)
+            result = work.tile([P, V], F32, name="result")
+            nc.vector.tensor_tensor(result[:], diff[:], qn[:], ALU.mult)
+            nc.sync.dma_start(out=out[b * P : (b + 1) * P, :], in_=result[:])

@@ -22,7 +22,9 @@ PASSES = K // (P * PACK)
 BLOCKS = S // P
 HALF = S // 2
 LIST_ROWS = 16
-INV = 1.0 / 0.6
+CHUNKS = V // P
+FAR = 1e25
+SCALAR_BLOCKS = (1,)
 
 
 def tile_picked_ytsneg_grad_p_kernel(
@@ -31,106 +33,141 @@ def tile_picked_ytsneg_grad_p_kernel(
     nc = tc.nc
     with ExitStack() as ctx:
         keep = ctx.enter_context(tc.tile_pool(name="keep", bufs=1))
+        reuse = ctx.enter_context(tc.tile_pool(name="reuse", bufs=1))
         work = ctx.enter_context(tc.tile_pool(name="work", bufs=4))
-        psum_h = ctx.enter_context(tc.psum_pool(name="psum_h", bufs=3))
-        psum_y = ctx.enter_context(tc.psum_pool(name="psum_y", bufs=3))
-        psum_n = ctx.enter_context(tc.psum_pool(name="psum_n", bufs=1))
+        psum_h = ctx.enter_context(tc.psum_pool(name="psum_h", bufs=2))
+        psum_y = ctx.enter_context(tc.psum_pool(name="psum_y", bufs=2))
+        psum_d = ctx.enter_context(tc.psum_pool(name="psum_d", bufs=4))
+
+        def shared(shape, dtype, place, name):
+            return reuse.tile(shape, dtype, tag=place, name=name, align_bytes=64)
 
         offs_sb = keep.tile([P, S // LIST_ROWS], U16, name="offs_sb")
         lmk_sb = keep.tile([P, V // LIST_ROWS], U16, name="lmk_sb")
-        x_scale_table = keep.tile([P, T], U8, name="x_scale_table")
-        e_scale_table = keep.tile([P, W], U8, name="e_scale_table")
-        nn_table = keep.tile([P, W], F32, name="nn_table")
+        x_scale_table = shared([P, T], U8, "d", "x_scale_table")
+        e_scale_table = shared([P, W], U8, "g", "e_scale_table")
+        nn_table = shared([P, W], F32, "f", "nn_table")
+        rows = keep.tile([P, P], F32, name="rows")
         nc.vector.memset(x_scale_table[:].bitcast(I32), 0)
+        nc.vector.memset(rows[:], 0.0)
         nc.vector.memset(e_scale_table[:].bitcast(I32), 0)
-        nc.vector.memset(nn_table[:], 0.0)
-        own_rows = keep.tile([P, P], F32, name="own_rows")
-        nc.vector.memset(own_rows[:], 0.0)
+        nc.gpsimd.memset(nn_table[:], 0.0)
+        ident = keep.tile([P, P], F32, name="ident")
+        make_identity(nc, ident[:])
 
-        warm = keep.tile([P, 8], F32, name="warm")
-        nc.vector.memset(warm[:], 1.0)
-        nc.scalar.activation(warm[:, 1:2], warm[:, 0:1], ACT.Abs_reciprocal_sqrt)
+        def load_w(g, place):
+            tile = shared([P, PACK, H], F32, place, "w_raw%d" % g)
+            k_rows = w1[g * P * PACK : (g + 1) * P * PACK, :]
+            nc.sync.dma_start(out=tile[:], in_=k_rows.rearrange("(p j) c -> p j c", j=PACK))
+            return tile
 
-        w_raw = [keep.tile([P, PACK, H], F32, name="w_raw%d" % g) for g in range(PASSES)]
-        x_table = [keep.tile([P, T], I32, name="x_table%d" % g) for g in range(PASSES)]
-        e_table = keep.tile([P, W], I32, name="e_table")
-        one_sb = keep.tile([P, V], F32, name="one_sb")
-        pij_sb = [keep.tile([P, V], F32, name="pij_sb%d" % b) for b in range(BLOCKS)]
+        def load_words(words, place, name):
+            tile = shared([P, T], I32, place, name)
+            nc.sync.dma_start(out=tile[:], in_=words.rearrange("p n t -> p (n t)").bitcast(I32))
+            return tile
 
-        def load_w(g):
-            rows = w1[g * P * PACK : (g + 1) * P * PACK, :]
-            nc.sync.dma_start(out=w_raw[g][:], in_=rows.rearrange("(p j) c -> p j c", j=PACK))
-
-        load_w(0)
+        nc.sync.dma_start(offs_sb[:], offs)
+        nc.sync.dma_start(lmk_sb[:], lmk)
+        w_raw = [load_w(0, "a")]
+        warm_in = shared([P, 1], F32, "b", "warm_in")
+        warm_out = shared([P, 1], F32, "c", "warm_out")
+        nc.vector.memset(warm_in[:], 1.0)
+        nc.scalar.activation(warm_out[:], warm_in[:], ACT.Abs_reciprocal_sqrt)
         for q in range(4):
             nc.sync.dma_start(
                 out=x_scale_table[32 * q : 32 * q + 4 * PASSES, :].bitcast(I32),
                 in_=x_scales[:, 4 * q : 4 * q + 4, :].bitcast(I32),
             )
-        nc.sync.dma_start(offs_sb[:], offs)
-        nc.sync.dma_start(lmk_sb[:], lmk)
-        load_w(1)
-        for g in range(PASSES):
-            nc.sync.dma_start(out=x_table[g][:], in_=x_words[g].rearrange("p n t -> p (n t)").bitcast(I32))
-        nc.sync.dma_start(out=e_table[:], in_=e_words[0].rearrange("p n t -> p (n t)").bitcast(I32))
-        nc.sync.dma_start(out=one_sb[:], in_=one)
-        for b in range(BLOCKS):
-            nc.sync.dma_start(out=pij_sb[b][:], in_=pij[b * P : (b + 1) * P, :])
-        nc.gpsimd.dma_start(out=nn_table[0:1, :], in_=nn[0:1, :])
-        nc.gpsimd.dma_start(out=own_rows[0:BLOCKS, :], in_=own.rearrange("(b p) o -> b (p o)", p=P))
+        nc.sync.dma_start(out=rows[0:BLOCKS, :], in_=own.rearrange("(b p) o -> b (p o)", p=P))
+        nc.sync.dma_start(out=rows[BLOCKS : BLOCKS + CHUNKS, :], in_=one[0:1, :].rearrange("o (j p) -> (o j) p", p=P))
+        w_raw.append(load_w(1, "b"))
+        nc.sync.dma_start(out=nn_table[0:1, :], in_=nn[0:1, :])
         for q in range(4):
-            nc.gpsimd.dma_start(
+            nc.sync.dma_start(
                 out=e_scale_table[32 * q : 32 * q + 4, :].bitcast(I32),
                 in_=e_scales[0, 4 * q : 4 * q + 4, :].bitcast(I32),
             )
+        x_table = [load_words(x_words[0], "c", "x_table0")]
 
-        ident = keep.tile([P, P], F32, name="ident")
-        make_identity(nc, ident[:])
-
-        w_codes, w_scales = [], []
-        for g in range(PASSES):
-            grouped = keep.tile([P, PACK * H], BF16, name="w_grouped%d" % g, align_bytes=64)
+        def quantize_w(g, grouped_place, codes_place):
+            grouped = shared([P, PACK * H], BF16, grouped_place, "w_grouped%d" % g)
             nc.scalar.copy(
                 out=grouped[:].rearrange("p (t m j) -> p m j t", t=PACK, j=PACK),
                 in_=w_raw[g][:].rearrange("p j (m t) -> p m j t", t=PACK),
             )
-            codes = keep.tile([P, H], U32, name="w_codes%d" % g, align_bytes=64)
+            codes = shared([P, H], U32, codes_place, "w_codes%d" % g)
             scales = keep.tile([P, H], U8, name="w_scales%d" % g, align_bytes=64)
             nc.vector.quantize_mx(out=codes[:].bitcast(FP8X4), scales=scales[:], in_=grouped[:])
-            w_codes.append(codes)
-            w_scales.append(scales)
+            return codes, scales
+
+        def pick_words(table, offsets, name, places):
+            halves = []
+            for half in range(2):
+                picked = shared([P, HALF], U32, places[half], "%s%d" % (name, half))
+                entries = slice(half * HALF // LIST_ROWS, (half + 1) * HALF // LIST_ROWS)
+                nc.vector.tensor_copy(picked[:], table[:].bitcast(U32).indirect(offsets[:, entries]))
+                halves.append(picked)
+            return halves
 
         x_scale_picked = keep.tile([P, S], U8, name="x_scale_picked", align_bytes=64)
         nc.vector.tensor_copy(x_scale_picked[:], x_scale_table[:].indirect(offs_sb[:]))
-        e_scale_picked = keep.tile([P, V], U8, name="e_scale_picked", align_bytes=64)
-        nc.vector.tensor_copy(e_scale_picked[:], e_scale_table[:].indirect(lmk_sb[:]))
 
-        nn_row = keep.tile([P, V], F32, name="nn_row")
+        rows_turned = psum_d.tile([P, P], F32, name="den")
+        nc.tensor.transpose(rows_turned[:], rows[:], ident[:])
+        cols = keep.tile([P, BLOCKS + CHUNKS], F32, name="cols")
+        nc.scalar.copy(out=cols[:], in_=rows_turned[:, 0 : BLOCKS + CHUNKS])
+        one_col = cols[:, BLOCKS : BLOCKS + CHUNKS]
+        massless = keep.tile([P, CHUNKS], F32, name="massless")
+        nc.gpsimd.tensor_scalar(massless[:], one_col, 0.0, None, ALU.is_equal)
+        mass = keep.tile([P, CHUNKS], F32, name="mass")
+        nc.gpsimd.tensor_tensor(mass[:], one_col, massless[:], ALU.add)
+        inv_mass = keep.tile([P, CHUNKS], F32, name="inv_mass")
+        nc.vector.reciprocal(inv_mass[:], mass[:])
+        live = keep.tile([P, CHUNKS], F32, name="live")
+        nc.gpsimd.tensor_scalar(live[:], massless[:], -1.0, 1.0, ALU.mult, ALU.add)
+        far_term = keep.tile([P, CHUNKS], F32, name="far_term")
+        nc.gpsimd.tensor_scalar(far_term[:], massless[:], FAR, 0.0, ALU.mult, ALU.add)
+        factor = keep.tile([P, CHUNKS], F32, name="factor")
+        nc.gpsimd.tensor_tensor(factor[:], live[:], inv_mass[:], ALU.mult)
+        y_factor = keep.tile([P, CHUNKS], F32, name="y_factor")
+        nc.gpsimd.tensor_scalar(y_factor[:], factor[:], -0.6, 0.0, ALU.mult, ALU.add)
+
+        w_mx = [quantize_w(0, "e", "d")]
+        nn_row = shared([P, V], F32, "e", "nn_row")
         nc.vector.tensor_copy(nn_row[:], nn_table[:].indirect(lmk_sb[:]))
-        nn_turned = psum_n.tile([P, V // P, P], F32, name="nn_turned")
-        for j in range(V // P):
+        x_table.append(load_words(x_words[1], "a", "x_table1"))
+        x_picked = [pick_words(x_table[0], offs_sb, "x_picked0", ("f", "i"))]
+        w_mx.append(quantize_w(1, "h", "c"))
+        e_table = load_words(e_words[0], "b", "e_table")
+        pij_sb = shared([P, BLOCKS, V], F32, "h", "pij_sb")
+        for b in range(BLOCKS):
+            nc.sync.dma_start(out=pij_sb[:, b, :], in_=pij[b * P : (b + 1) * P, :])
+        nn_turned = psum_d.tile([P, CHUNKS, P], F32, name="den")
+        for j in range(CHUNKS):
             nc.tensor.transpose(nn_turned[:, j, :], nn_row[:, j * P : (j + 1) * P], ident[:])
-        nn_col = keep.tile([P, V // P], F32, name="nn_col")
-        nc.vector.tensor_scalar(nn_col[:], nn_turned[:, :, 0], -INV, -INV, ALU.mult, ALU.add)
-        nn_spread = psum_n.tile([P, V], F32, name="nn_spread")
-        for j in range(V // P):
-            nc.tensor.transpose(
-                nn_spread[:, j * P : (j + 1) * P], nn_col[:, j : j + 1].to_broadcast([P, P]), ident[:]
-            )
-        nn_term = keep.tile([P, V], F32, name="nn_term")
-        nc.scalar.copy(out=nn_term[:], in_=nn_spread[:])
-        own_term = keep.tile([P, BLOCKS], F32, name="own_term")
-        own_turned = psum_h.tile([P, PACK, P], F32, name="h_acc")
-        nc.tensor.transpose(own_turned[:, 0, :], own_rows[:], ident[:])
-        nc.vector.tensor_scalar(own_term[:], own_turned[:, 0, 0:BLOCKS], -INV, None, ALU.mult)
+        nn_col = keep.tile([P, CHUNKS], F32, name="nn_col")
+        nc.scalar.activation(nn_col[:], nn_turned[:, :, 0], ACT.Copy, bias=1.0)
+        nn_scaled = keep.tile([P, CHUNKS], F32, name="nn_scaled")
+        nc.gpsimd.tensor_tensor(nn_scaled[:], nn_col[:], factor[:], ALU.mult)
+        nn_term = keep.tile([P, CHUNKS], F32, name="nn_term")
+        nc.gpsimd.tensor_tensor(nn_term[:], nn_scaled[:], far_term[:], ALU.add)
 
-        x_picked = {}
-        for g in range(PASSES):
-            for half in range(2):
-                picked = keep.tile([P, HALF], U32, name="x_picked%d%d" % (g, half), align_bytes=64)
-                cols = slice(half * HALF // LIST_ROWS, (half + 1) * HALF // LIST_ROWS)
-                nc.vector.tensor_copy(picked[:], x_table[g][:].bitcast(U32).indirect(offs_sb[:, cols]))
-                x_picked[g, half] = picked
+        own_spread = psum_d.tile([P, S], F32, name="den")
+        for b in range(BLOCKS):
+            nc.tensor.transpose(
+                own_spread[:, b * P : (b + 1) * P], cols[:, b : b + 1].to_broadcast([P, P]), ident[:]
+            )
+        norms = [keep.tile([P, S], F32, name="norms%d" % j) for j in range(CHUNKS)]
+        for j in range(CHUNKS):
+            nc.scalar.activation(
+                norms[j][:], own_spread[:], ACT.Identity, scale=factor[:, j : j + 1], bias=nn_term[:, j : j + 1]
+            )
+
+        x_picked.append(pick_words(x_table[1], offs_sb, "x_picked1", ("j", "k")))
+
+        e_scale_picked = shared([P, V], U8, "a", "e_scale_picked")
+        nc.vector.tensor_copy(e_scale_picked[:], e_scale_table[:].indirect(lmk_sb[:]))
+        e_picked = pick_words(e_table, lmk_sb, "e_picked", ("g", "l"))
 
         h_codes, h_scales = [], []
         for b in range(BLOCKS):
@@ -140,9 +177,9 @@ def tile_picked_ytsneg_grad_p_kernel(
                 for g in range(PASSES):
                     nc.tensor.matmul_mx(
                         out=h_acc[:, t, :],
-                        lhsT=w_codes[g][:, t * P : (t + 1) * P].bitcast(FP8X4),
-                        lhsT_scale=w_scales[g][:, t * P : (t + 1) * P],
-                        rhs=x_picked[g, half][:, first : first + P].bitcast(FP8X4),
+                        lhsT=w_mx[g][0][:, t * P : (t + 1) * P].bitcast(FP8X4),
+                        lhsT_scale=w_mx[g][1][:, t * P : (t + 1) * P],
+                        rhs=x_picked[g][half][:, first : first + P].bitcast(FP8X4),
                         rhs_scale=x_scale_picked[4 * g : P, b * P : (b + 1) * P],
                         start=(g == 0),
                         stop=(g == PASSES - 1),
@@ -151,45 +188,58 @@ def tile_picked_ytsneg_grad_p_kernel(
             nc.scalar.copy(
                 out=h_grouped[:].rearrange("p (n t) -> p n t", t=PACK), in_=h_acc[:].rearrange("p t n -> p n t")
             )
-            codes = work.tile([P, P], U32, name="h_codes", align_bytes=64)
+            codes = shared([P, P], U32, ("b", "m", "n", "o")[b], "h_codes%d" % b)
             scales = work.tile([P, P], U8, name="h_scales", align_bytes=64)
             nc.vector.quantize_mx(out=codes[:].bitcast(FP8X4), scales=scales[:], in_=h_grouped[:])
             h_codes.append(codes)
             h_scales.append(scales)
 
-        e_picked = keep.tile([P, V], U32, name="e_picked", align_bytes=64)
-        nc.vector.tensor_copy(e_picked[:], e_table[:].bitcast(U32).indirect(lmk_sb[:]))
-
         for b in range(BLOCKS):
-            y_acc = psum_y.tile([P, V], F32, name="y_acc")
-            nc.tensor.matmul_mx(
-                out=y_acc[:],
-                lhsT=h_codes[b][:].bitcast(FP8X4),
-                lhsT_scale=h_scales[b][:],
-                rhs=e_picked[:].bitcast(FP8X4),
-                rhs_scale=e_scale_picked[:],
-                start=True,
-                stop=True,
-            )
-            den = work.tile([P, V], F32, name="den")
-            nc.vector.scalar_tensor_tensor(den[:], y_acc[:], own_term[:, b : b + 1], nn_term[:], ALU.add, ALU.add)
-            sign = work.tile([P, V], F32, name="sign")
-            nc.scalar.activation(sign[:], den[:], ACT.Sign, scale=-1.0)
+            tokens = slice(b * P, (b + 1) * P)
+            y_acc = psum_y.tile([P, CHUNKS, P], F32, name="y_acc")
+            for j in range(CHUNKS):
+                half, first = divmod(j * P, HALF)
+                nc.tensor.matmul_mx(
+                    out=y_acc[:, j, :],
+                    lhsT=e_picked[half][:, first : first + P].bitcast(FP8X4),
+                    lhsT_scale=e_scale_picked[:, j * P : (j + 1) * P],
+                    rhs=h_codes[b][:].bitcast(FP8X4),
+                    rhs_scale=h_scales[b][:],
+                    start=True,
+                    stop=True,
+                )
+            den_t = work.tile([P, CHUNKS, P], F32, name="den_t")
+            den = psum_d.tile([P, V], F32, name="den")
+            for j in range(CHUNKS):
+                if b in SCALAR_BLOCKS:
+                    nc.scalar.activation(den_t[:, j, :], y_acc[:, j, :], ACT.Copy, scale=y_factor[:, j : j + 1])
+                else:
+                    nc.vector.scalar_tensor_tensor(
+                        den_t[:, j, :], y_acc[:, j, :], y_factor[:, j : j + 1], norms[j][:, tokens], ALU.mult, ALU.add
+                    )
+            for j in range(CHUNKS):
+                marks = slice(j * P, (j + 1) * P)
+                if b in SCALAR_BLOCKS:
+                    nc.tensor.matmul(den[:, marks], norms[j][:, tokens], ident[:], start=True, stop=False, is_transpose=True)
+                    nc.tensor.matmul(den[:, marks], den_t[:, j, :], ident[:], start=False, stop=True, is_transpose=True)
+                else:
+                    nc.tensor.transpose(den[:, marks], den_t[:, j, :], ident[:])
             root = work.tile([P, V], F32, name="root")
-            nc.scalar.activation(root[:], den[:], ACT.Abs_reciprocal_sqrt, scale=0.6)
+            nc.scalar.activation(root[:], den[:], ACT.Abs_reciprocal_sqrt)
             inv_abs = work.tile([P, V], F32, name="inv_abs")
             nc.scalar.activation(inv_abs[:], root[:], ACT.Square)
-            signed_one = work.tile([P, V], F32, name="signed_one")
-            nc.vector.tensor_tensor(signed_one[:], sign[:], one_sb[:], ALU.mult)
-            qn = work.tile([P, V], F32, name="qn")
-            stats = work.tile([P, 8], F32, name="stats")
+            inv_square = work.tile([P, V], F32, name="inv_square")
+            nc.scalar.activation(inv_square[:], inv_abs[:], ACT.Square)
+            pull = work.tile([P, V], F32, name="pull")
+            nc.vector.tensor_tensor(pull[:], den[:], pij_sb[:, b, :], ALU.mult)
+            share = work.tile([P, V], F32, name="share")
+            stats = work.tile([P, 2], F32, name="stats")
             nc.vector.scalar_tensor_tensor(
-                qn[:], signed_one[:], 1.0, inv_abs[:], ALU.mult, ALU.mult, accum_out=stats[:, 0:1]
+                share[:], den[:], 1.0 / V, inv_square[:], ALU.mult, ALU.mult, accum_out=stats[:, 0:1]
             )
-            nc.vector.tensor_scalar(stats[:, 1:2], stats[:, 0:1], -1.0 / V, None, ALU.mult)
-            nc.vector.reciprocal(stats[:, 2:3], stats[:, 1:2])
-            diff = work.tile([P, V], F32, name="diff")
-            nc.vector.scalar_tensor_tensor(diff[:], qn[:], stats[:, 2:3], pij_sb[b][:], ALU.mult, ALU.add)
+            nc.vector.reciprocal(stats[:, 1:2], stats[:, 0:1])
             result = work.tile([P, V], F32, name="result")
-            nc.vector.tensor_tensor(result[:], diff[:], qn[:], ALU.mult)
+            nc.vector.scalar_tensor_tensor(
+                result[:], pull[:], stats[:, 1:2], inv_square[:], ALU.subtract, ALU.mult
+            )
             nc.sync.dma_start(out=out[b * P : (b + 1) * P, :], in_=result[:])

from contextlib import ExitStack

import concourse.mybir as mybir
from concourse.masks import make_identity

K, T, S, H, V, W = 1024, 2048, 512, 512, 512, 2048
FLOPS = 2 * K * H * S + 2 * H * S * V

F32 = mybir.dt.float32
BF16 = mybir.dt.bfloat16
I32 = mybir.dt.int32
U32 = mybir.dt.uint32
U16 = mybir.dt.uint16
U8 = mybir.dt.uint8
FP8X4 = mybir.dt.float8_e4m3fn_x4
ALU = mybir.AluOpType
ACT = mybir.ActivationFunctionType

P = 128
PACK = 4
PASSES = K // (P * PACK)
BLOCKS = S // P
HALF = S // 2
LIST_ROWS = 16
CHUNKS = V // P
FAR = 1e25
SCALAR_BLOCKS = (1,)


def tile_picked_ytsneg_grad_p_kernel(
    tc, x_words, x_scales, w1, e_words, e_scales, nn, own, one, pij, offs, lmk, out
):
    nc = tc.nc
    with ExitStack() as ctx:
        keep = ctx.enter_context(tc.tile_pool(name="keep", bufs=1))
        reuse = ctx.enter_context(tc.tile_pool(name="reuse", bufs=1))
        work = ctx.enter_context(tc.tile_pool(name="work", bufs=4))
        psum_h = ctx.enter_context(tc.psum_pool(name="psum_h", bufs=2))
        psum_y = ctx.enter_context(tc.psum_pool(name="psum_y", bufs=2))
        psum_d = ctx.enter_context(tc.psum_pool(name="psum_d", bufs=4))

        def shared(shape, dtype, place, name):
            return reuse.tile(shape, dtype, tag=place, name=name, align_bytes=64)

        offs_sb = keep.tile([P, S // LIST_ROWS], U16, name="offs_sb")
        lmk_sb = keep.tile([P, V // LIST_ROWS], U16, name="lmk_sb")
        x_scale_table = shared([P, T], U8, "d", "x_scale_table")
        e_scale_table = shared([P, W], U8, "g", "e_scale_table")
        nn_table = shared([P, W], F32, "f", "nn_table")
        rows = keep.tile([P, P], F32, name="rows")
        nc.vector.memset(x_scale_table[:].bitcast(I32), 0)
        nc.vector.memset(rows[:], 0.0)
        nc.vector.memset(e_scale_table[:].bitcast(I32), 0)
        nc.gpsimd.memset(nn_table[:], 0.0)
        ident = keep.tile([P, P], F32, name="ident")
        make_identity(nc, ident[:])

        def load_w(g, place):
            tile = shared([P, PACK, H], F32, place, "w_raw%d" % g)
            k_rows = w1[g * P * PACK : (g + 1) * P * PACK, :]
            nc.sync.dma_start(out=tile[:], in_=k_rows.rearrange("(p j) c -> p j c", j=PACK))
            return tile

        def load_words(words, place, name):
            tile = shared([P, T], I32, place, name)
            nc.sync.dma_start(out=tile[:], in_=words.rearrange("p n t -> p (n t)").bitcast(I32))
            return tile

        nc.sync.dma_start(offs_sb[:], offs)
        nc.sync.dma_start(lmk_sb[:], lmk)
        w_raw = [load_w(0, "a")]
        warm_in = shared([P, 1], F32, "b", "warm_in")
        warm_out = shared([P, 1], F32, "c", "warm_out")
        nc.vector.memset(warm_in[:], 1.0)
        nc.scalar.activation(warm_out[:], warm_in[:], ACT.Abs_reciprocal_sqrt)
        for q in range(4):
            nc.sync.dma_start(
                out=x_scale_table[32 * q : 32 * q + 4 * PASSES, :].bitcast(I32),
                in_=x_scales[:, 4 * q : 4 * q + 4, :].bitcast(I32),
            )
        nc.sync.dma_start(out=rows[0:BLOCKS, :], in_=own.rearrange("(b p) o -> b (p o)", p=P))
        nc.sync.dma_start(out=rows[BLOCKS : BLOCKS + CHUNKS, :], in_=one[0:1, :].rearrange("o (j p) -> (o j) p", p=P))
        w_raw.append(load_w(1, "b"))
        nc.sync.dma_start(out=nn_table[0:1, :], in_=nn[0:1, :])
        for q in range(4):
            nc.sync.dma_start(
                out=e_scale_table[32 * q : 32 * q + 4, :].bitcast(I32),
                in_=e_scales[0, 4 * q : 4 * q + 4, :].bitcast(I32),
            )
        x_table = [load_words(x_words[0], "c", "x_table0")]

        def quantize_w(g, grouped_place, codes_place):
            grouped = shared([P, PACK * H], BF16, grouped_place, "w_grouped%d" % g)
            nc.scalar.copy(
                out=grouped[:].rearrange("p (t m j) -> p m j t", t=PACK, j=PACK),
                in_=w_raw[g][:].rearrange("p j (m t) -> p m j t", t=PACK),
            )
            codes = shared([P, H], U32, codes_place, "w_codes%d" % g)
            scales = keep.tile([P, H], U8, name="w_scales%d" % g, align_bytes=64)
            nc.vector.quantize_mx(out=codes[:].bitcast(FP8X4), scales=scales[:], in_=grouped[:])
            return codes, scales

        def pick_words(table, offsets, name, places):
            halves = []
            for half in range(2):
                picked = shared([P, HALF], U32, places[half], "%s%d" % (name, half))
                entries = slice(half * HALF // LIST_ROWS, (half + 1) * HALF // LIST_ROWS)
                nc.vector.tensor_copy(picked[:], table[:].bitcast(U32).indirect(offsets[:, entries]))
                halves.append(picked)
            return halves

        x_scale_picked = keep.tile([P, S], U8, name="x_scale_picked", align_bytes=64)
        nc.vector.tensor_copy(x_scale_picked[:], x_scale_table[:].indirect(offs_sb[:]))

        rows_turned = psum_d.tile([P, P], F32, name="den")
        nc.tensor.transpose(rows_turned[:], rows[:], ident[:])
        cols = keep.tile([P, BLOCKS + CHUNKS], F32, name="cols")
        nc.scalar.copy(out=cols[:], in_=rows_turned[:, 0 : BLOCKS + CHUNKS])
        one_col = cols[:, BLOCKS : BLOCKS + CHUNKS]
        massless = keep.tile([P, CHUNKS], F32, name="massless")
        nc.gpsimd.tensor_scalar(massless[:], one_col, 0.0, None, ALU.is_equal)
        mass = keep.tile([P, CHUNKS], F32, name="mass")
        nc.gpsimd.tensor_tensor(mass[:], one_col, massless[:], ALU.add)
        inv_mass = keep.tile([P, CHUNKS], F32, name="inv_mass")
        nc.vector.reciprocal(inv_mass[:], mass[:])
        live = keep.tile([P, CHUNKS], F32, name="live")
        nc.gpsimd.tensor_scalar(live[:], massless[:], -1.0, 1.0, ALU.mult, ALU.add)
        far_term = keep.tile([P, CHUNKS], F32, name="far_term")
        nc.gpsimd.tensor_scalar(far_term[:], massless[:], FAR, 0.0, ALU.mult, ALU.add)
        factor = keep.tile([P, CHUNKS], F32, name="factor")
        nc.gpsimd.tensor_tensor(factor[:], live[:], inv_mass[:], ALU.mult)
        y_factor = keep.tile([P, CHUNKS], F32, name="y_factor")
        nc.gpsimd.tensor_scalar(y_factor[:], factor[:], -0.6, 0.0, ALU.mult, ALU.add)

        w_mx = [quantize_w(0, "e", "d")]
        nn_row = shared([P, V], F32, "e", "nn_row")
        nc.vector.tensor_copy(nn_row[:], nn_table[:].indirect(lmk_sb[:]))
        x_table.append(load_words(x_words[1], "a", "x_table1"))
        x_picked = [pick_words(x_table[0], offs_sb, "x_picked0", ("f", "i"))]
        w_mx.append(quantize_w(1, "h", "c"))
        e_table = load_words(e_words[0], "b", "e_table")
        pij_sb = shared([P, BLOCKS, V], F32, "h", "pij_sb")
        for b in range(BLOCKS):
            nc.sync.dma_start(out=pij_sb[:, b, :], in_=pij[b * P : (b + 1) * P, :])
        nn_turned = psum_d.tile([P, CHUNKS, P], F32, name="den")
        for j in range(CHUNKS):
            nc.tensor.transpose(nn_turned[:, j, :], nn_row[:, j * P : (j + 1) * P], ident[:])
        nn_col = keep.tile([P, CHUNKS], F32, name="nn_col")
        nc.scalar.activation(nn_col[:], nn_turned[:, :, 0], ACT.Copy, bias=1.0)
        nn_scaled = keep.tile([P, CHUNKS], F32, name="nn_scaled")
        nc.gpsimd.tensor_tensor(nn_scaled[:], nn_col[:], factor[:], ALU.mult)
        nn_term = keep.tile([P, CHUNKS], F32, name="nn_term")
        nc.gpsimd.tensor_tensor(nn_term[:], nn_scaled[:], far_term[:], ALU.add)

        own_spread = psum_d.tile([P, S], F32, name="den")
        for b in range(BLOCKS):
            nc.tensor.transpose(
                own_spread[:, b * P : (b + 1) * P], cols[:, b : b + 1].to_broadcast([P, P]), ident[:]
            )
        norms = [keep.tile([P, S], F32, name="norms%d" % j) for j in range(CHUNKS)]
        for j in range(CHUNKS):
            nc.scalar.activation(
                norms[j][:], own_spread[:], ACT.Identity, scale=factor[:, j : j + 1], bias=nn_term[:, j : j + 1]
            )

        x_picked.append(pick_words(x_table[1], offs_sb, "x_picked1", ("j", "k")))

        e_scale_picked = shared([P, V], U8, "a", "e_scale_picked")
        nc.vector.tensor_copy(e_scale_picked[:], e_scale_table[:].indirect(lmk_sb[:]))
        e_picked = pick_words(e_table, lmk_sb, "e_picked", ("g", "l"))

        h_codes, h_scales = [], []
        for b in range(BLOCKS):
            half, first = divmod(b * P, HALF)
            h_acc = psum_h.tile([P, PACK, P], F32, name="h_acc")
            for t in range(PACK):
                for g in range(PASSES):
                    nc.tensor.matmul_mx(
                        out=h_acc[:, t, :],
                        lhsT=w_mx[g][0][:, t * P : (t + 1) * P].bitcast(FP8X4),
                        lhsT_scale=w_mx[g][1][:, t * P : (t + 1) * P],
                        rhs=x_picked[g][half][:, first : first + P].bitcast(FP8X4),
                        rhs_scale=x_scale_picked[4 * g : P, b * P : (b + 1) * P],
                        start=(g == 0),
                        stop=(g == PASSES - 1),
                    )
            h_grouped = work.tile([P, P * PACK], BF16, name="h_grouped", align_bytes=64)
            nc.scalar.copy(
                out=h_grouped[:].rearrange("p (n t) -> p n t", t=PACK), in_=h_acc[:].rearrange("p t n -> p n t")
            )
            codes = shared([P, P], U32, ("b", "m", "n", "o")[b], "h_codes%d" % b)
            scales = work.tile([P, P], U8, name="h_scales", align_bytes=64)
            nc.vector.quantize_mx(out=codes[:].bitcast(FP8X4), scales=scales[:], in_=h_grouped[:])
            h_codes.append(codes)
            h_scales.append(scales)

        for b in range(BLOCKS):
            tokens = slice(b * P, (b + 1) * P)
            y_acc = psum_y.tile([P, CHUNKS, P], F32, name="y_acc")
            for j in range(CHUNKS):
                half, first = divmod(j * P, HALF)
                nc.tensor.matmul_mx(
                    out=y_acc[:, j, :],
                    lhsT=e_picked[half][:, first : first + P].bitcast(FP8X4),
                    lhsT_scale=e_scale_picked[:, j * P : (j + 1) * P],
                    rhs=h_codes[b][:].bitcast(FP8X4),
                    rhs_scale=h_scales[b][:],
                    start=True,
                    stop=True,
                )
            den_t = work.tile([P, CHUNKS, P], F32, name="den_t")
            den = psum_d.tile([P, V], F32, name="den")
            for j in range(CHUNKS):
                if b in SCALAR_BLOCKS:
                    nc.scalar.activation(den_t[:, j, :], y_acc[:, j, :], ACT.Copy, scale=y_factor[:, j : j + 1])
                else:
                    nc.vector.scalar_tensor_tensor(
                        den_t[:, j, :], y_acc[:, j, :], y_factor[:, j : j + 1], norms[j][:, tokens], ALU.mult, ALU.add
                    )
            for j in range(CHUNKS):
                marks = slice(j * P, (j + 1) * P)
                if b in SCALAR_BLOCKS:
                    nc.tensor.matmul(den[:, marks], norms[j][:, tokens], ident[:], start=True, stop=False, is_transpose=True)
                    nc.tensor.matmul(den[:, marks], den_t[:, j, :], ident[:], start=False, stop=True, is_transpose=True)
                else:
                    nc.tensor.transpose(den[:, marks], den_t[:, j, :], ident[:])
            root = work.tile([P, V], F32, name="root")
            nc.scalar.activation(root[:], den[:], ACT.Abs_reciprocal_sqrt)
            inv_abs = work.tile([P, V], F32, name="inv_abs")
            nc.scalar.activation(inv_abs[:], root[:], ACT.Square)
            inv_square = work.tile([P, V], F32, name="inv_square")
            nc.scalar.activation(inv_square[:], inv_abs[:], ACT.Square)
            pull = work.tile([P, V], F32, name="pull")
            nc.vector.tensor_tensor(pull[:], den[:], pij_sb[:, b, :], ALU.mult)
            share = work.tile([P, V], F32, name="share")
            stats = work.tile([P, 2], F32, name="stats")
            nc.vector.scalar_tensor_tensor(
                share[:], den[:], 1.0 / V, inv_square[:], ALU.mult, ALU.mult, accum_out=stats[:, 0:1]
            )
            nc.vector.reciprocal(stats[:, 1:2], stats[:, 0:1])
            result = work.tile([P, V], F32, name="result")
            nc.vector.scalar_tensor_tensor(
                result[:], pull[:], stats[:, 1:2], inv_square[:], ALU.subtract, ALU.mult
            )
            nc.sync.dma_start(out=out[b * P : (b + 1) * P, :], in_=result[:])
